import numpy as np
import ml_dtypes


def mxq(x, axis, fmt="e4m3"):
    dtype, down = {"e4m3": (ml_dtypes.float8_e4m3fn, 7), "e5m2": (ml_dtypes.float8_e5m2, 14)}[fmt]
    v = np.moveaxis(np.asarray(x, np.float32).astype(ml_dtypes.bfloat16).astype(np.float64), axis, -1)
    blocks = v.reshape(v.shape[:-1] + (-1, 32))
    amax = np.abs(blocks).max(-1, keepdims=True)
    byte = np.maximum(np.where(amax > 0, np.frexp(amax)[1] - 1 + 127, 0) - down, 1)
    scale = np.exp2(byte - 127.0)
    codes = (blocks / scale).astype(np.float32).astype(dtype).astype(np.float64)
    return np.moveaxis((codes * scale).reshape(v.shape), -1, axis)


WIDE = False


def mx_kscale(k):
    if not WIDE:
        return np.ones(k)
    levels = np.array([10, -10, 5, -5, 0])
    if k % 512:
        return np.exp2(np.random.permutation(np.resize(levels, k // 32))).repeat(32)
    a = np.empty((k // 512, 16))
    for p in range(k // 512):
        a[p, :8] = np.random.permutation(np.resize(levels, 8))
        for g in range(8):
            far = levels[np.abs(levels - a[p, g]) >= 10]
            a[p, g + 8] = far[np.random.randint(len(far))]
    return np.exp2(a.ravel()).repeat(32)


def f64(x):
    return np.asarray(x).astype(np.float64)


def striped(idx):
    return np.tile(idx.reshape(-1, 16).T, (8, 1)).astype(np.uint16)


def unstriped(offs):
    return offs[:16].T.reshape(-1).astype(np.int64)


def striped8(idx):
    return np.concatenate([x.reshape(-1, 16).T for x in idx]).astype(np.uint16)


def runs(offs, k):
    lists = np.stack([offs[16 * r : 16 * r + 16].T.reshape(-1) for r in range(8)]).astype(np.int64)
    return lists[np.arange(k) % 512 // 64]


def pack_weight(w):
    k, n = w.shape
    w = f64(np.asarray(w, np.float32).astype(ml_dtypes.bfloat16)).reshape(k // 32, 32, n)
    amax = np.abs(w).max(1)
    byte = np.clip(np.where(amax > 0, np.frexp(amax)[1] - 1 + 127 - 7, 1), 1, 254)
    scaled = (w * np.exp2(127.0 - byte)[:, None, :]).reshape(k, n).astype(np.float32)
    words = np.ascontiguousarray(scaled.reshape(k // 512, 128, 4, n).transpose(0, 1, 3, 2)).astype(ml_dtypes.float8_e4m3fn).view(np.uint8)
    return words, np.ascontiguousarray(byte.astype(np.uint8).reshape(k // 512, 16, n))


def unpack_weight(words, scales):
    g, p, n, _ = words.shape
    vals = np.ascontiguousarray(words).view(ml_dtypes.float8_e4m3fn).astype(np.float64) * np.repeat(np.exp2(scales.astype(np.float64) - 127.0), 8, axis=1)[..., None]
    return vals.transpose(0, 1, 3, 2).reshape(g * 512, n)


E2M1 = np.array([0.0, 0.5, 1.0, 1.5, 2.0, 3.0, 4.0, 6.0, -0.0, -0.5, -1.0, -1.5, -2.0, -3.0, -4.0, -6.0])


def pack_fp4(w):
    k, n = w.shape
    w = f64(np.asarray(w, np.float32).astype(ml_dtypes.bfloat16)).reshape(k // 32, 32, n)
    amax = np.abs(w).max(1)
    mant, ex = np.frexp(amax / 6.0)
    byte = np.clip(np.where(amax > 0, np.where(mant > 0.5, ex, ex - 1) + 127, 1), 1, 254)
    scaled = (w * np.exp2(127.0 - byte)[:, None, :]).reshape(k, n).astype(np.float32)
    c = np.ascontiguousarray(scaled.reshape(k // 512, 128, 4, n).transpose(0, 1, 3, 2)).astype(ml_dtypes.float4_e2m1fn).view(np.uint8) & 0xF
    words = (c[..., 0::2] | (c[..., 1::2] << 4)).reshape(k // 512, 128, 2 * n)
    return np.ascontiguousarray(words), np.ascontiguousarray(byte.astype(np.uint8).reshape(k // 512, 16, n))


def unpack_fp4(words, scales):
    g, _, n = scales.shape
    words = np.ascontiguousarray(words).reshape(g, 128, n, 2)
    nib = np.empty((g, 128, n, 4), np.uint8)
    nib[..., 0::2] = words & 0xF
    nib[..., 1::2] = words >> 4
    vals = E2M1[nib] * np.repeat(np.exp2(scales.astype(np.float64) - 127.0), 8, axis=1)[..., None]
    return vals.transpose(0, 1, 3, 2).reshape(g * 512, n)


def relu(v):
    return np.maximum(v, 0.0)

def planes(y):
    n, m = y.shape
    v = y.astype(np.float32).astype(ml_dtypes.bfloat16).astype(np.float64).reshape(n // 32, 32, m)
    top = np.abs(v).max(1)
    byte = np.clip(np.where(top > 0, np.frexp(top)[1] - 1 + 127 - 7, 1), 1, 254)
    codes = (v * np.exp2(127.0 - byte)[:, None, :]).reshape(n, m).astype(np.float32).astype(ml_dtypes.float8_e4m3fn).view(np.uint8)
    words = codes.reshape(n // 512, 128, 4, m).transpose(0, 1, 3, 2)
    return np.ascontiguousarray(words), np.ascontiguousarray(byte.astype(np.uint8).reshape(n // 512, 16, m))


K, T, S, H, U = 512, 2048, 512, 512, 1024


def setup_inputs():
    n = np.random.standard_normal
    s = mx_kscale(K)[:, None]
    u = mx_kscale(S)
    packed_xT = pack_weight(n((K, T)) * s)
    packed_w1 = pack_fp4(n((K, H)) / np.sqrt(K) / s)
    return {
        "x_words": packed_xT[0],
        "x_scales": packed_xT[1],
        "w1_words": packed_w1[0],
        "w1_scales": packed_w1[1],
        "ga": (np.random.uniform(0.5, 1.5, (H, 1)) * u[:, None]).astype(np.float32),
        "gb": (np.random.uniform(0.5, 1.5, (H, 1)) / u[:, None]).astype(np.float32),
        "offs": striped(np.random.permutation(T)[:S]),
        "n1": striped8(np.stack([np.random.permutation(S) for _ in range(8)])),
        "n2": striped8(np.stack([np.random.permutation(S) for _ in range(8)])),
        "n3": striped8(np.stack([np.random.permutation(U)[:S] for _ in range(8)])),
        "n4": striped8(np.stack([np.random.permutation(S) for _ in range(8)])),
        "n5": striped8(np.stack([np.random.permutation(U) for _ in range(8)])),
        "n6": striped8(np.stack([np.random.permutation(U) for _ in range(8)])),
    }


def reference(x_words, x_scales, w1_words, w1_scales, ga, gb, offs, n1, n2, n3, n4, n5, n6):
    xq = unpack_weight(x_words, x_scales)[:, unstriped(offs)]
    y = unpack_fp4(w1_words, w1_scales).T @ xq
    z = f64(ga) * (y[np.arange(H)[:, None], runs(n1, H)] - (y[np.arange(H)[:, None], runs(n2, H)]))
    nw = y - (relu(y[np.arange(H)[:, None], runs(n4, H)]))
    pg = np.zeros((H, U))
    pg[np.arange(H)[:, None], runs(n3, H)] = nw
    z2 = f64(gb) * pg
    s = 0.0625 * ((mxq(z, 0, "e4m3").T @ mxq(z2, 0, "e4m3")))
    out_0 = 0.75 * (s[np.arange(S)[:, None], runs(n5, S)] + s[np.arange(S)[:, None], runs(n6, S)]) - s
    return (out_0,) + planes(out_0)

@@ -1,0 +1,251 @@
+from contextlib import ExitStack
+
+import concourse.mybir as mybir
+
+F32 = mybir.dt.float32
+BF16 = mybir.dt.bfloat16
+I32 = mybir.dt.int32
+U32 = mybir.dt.uint32
+U16 = mybir.dt.uint16
+U8 = mybir.dt.uint8
+FP8X4 = mybir.dt.float8_e4m3fn_x4
+FP4X4 = mybir.dt.float4_e2m1fn_x4
+ADD = mybir.AluOpType.add
+SUB = mybir.AluOpType.subtract
+COPY = mybir.ActivationFunctionType.Copy
+RELU = mybir.ActivationFunctionType.Relu
+
+P = 128
+K, T, S, H, U = 512, 2048, 512, 512, 1024
+PACK = 4
+HALF = 256
+FLOPS = 2 * K * H * S + 2 * H * S * U
+
+
+def entries(tile, first, count):
+    return tile[:, first // 16 : (first + count) // 16]
+
+
+def tile_picked_selfgappagezlap_none_po_kernel(
+    tc, x_words, x_scales, w1_words, w1_scales, ga, gb, offs, n1, n2, n3, n4, n5, n6, out_0, out_1, out_2
+):
+    nc = tc.nc
+    with ExitStack() as ctx:
+        keep = ctx.enter_context(tc.tile_pool(name="keep", bufs=1))
+        ring = ctx.enter_context(tc.tile_pool(name="ring", bufs=3))
+        psum = ctx.enter_context(tc.psum_pool(name="psum", bufs=1))
+
+        def held(shape, dtype, name):
+            return keep.tile(shape, dtype, name=name, align_bytes=64)
+
+        lists = {}
+        for name, src in (("offs", offs), ("n4", n4), ("n3", n3), ("n1", n1), ("n2", n2), ("n5", n5), ("n6", n6)):
+            lists[name] = held(list(src.shape), U16, "list_" + name)
+
+        xw = held([P, T], U32, "xw")
+        xs = held([P, T], U8, "xs")
+        ww = held([P, 2 * H], U8, "ww")
+        ws = held([P, H], U8, "ws")
+        ga_sb = held([P, PACK], F32, "ga_sb")
+        gb_sb = held([P, PACK], F32, "gb_sb")
+        pg = [held([P, U], F32, "pg%d" % t) for t in range(PACK)]
+
+        nc.gpsimd.memset(xs[:].bitcast(I32), 0)
+        nc.gpsimd.memset(ws[:].bitcast(I32), 0)
+        nc.sync.dma_start(lists["offs"][:], offs)
+        nc.sync.dma_start(ww[:].bitcast(I32), w1_words[0].bitcast(I32))
+        nc.sync.dma_start(xw[:].bitcast(I32), x_words[0].rearrange("p n t -> p (n t)").bitcast(I32))
+        for q in range(4):
+            nc.scalar.dma_start(xs[32 * q : 32 * q + 4, :].bitcast(I32), x_scales[0][4 * q : 4 * q + 4, :].bitcast(I32))
+        for q in range(4):
+            queue = nc.scalar if q < 2 else nc.gpsimd
+            queue.dma_start(ws[32 * q : 32 * q + 4, :].bitcast(I32), w1_scales[0][4 * q : 4 * q + 4, :].bitcast(I32))
+        nc.sync.dma_start(lists["n4"][:], n4)
+        nc.sync.dma_start(lists["n3"][:], n3)
+        nc.sync.dma_start(ga_sb[:], ga.rearrange("(p t) o -> p (t o)", t=PACK))
+        nc.sync.dma_start(gb_sb[:], gb.rearrange("(p t) o -> p (t o)", t=PACK))
+        for name, src in (("n1", n1), ("n2", n2), ("n5", n5), ("n6", n6)):
+            nc.sync.dma_start(lists[name][:], src)
+        for t in range(PACK):
+            nc.vector.memset(pg[t][:], 0.0)
+
+        wd = held([P, 2 * H], U8, "wd")
+        nc.vector.tensor_copy(
+            wd[:].rearrange("p (t m b) -> p m t b", t=PACK, b=2), ww[:].rearrange("p (m t b) -> p m t b", t=PACK, b=2)
+        )
+        xqs = held([P, S], U8, "xqs")
+        nc.vector.tensor_copy(xqs[:], xs[:].indirect(lists["offs"][:]))
+        wsd = held([P, H], U8, "wsd")
+        nc.vector.tensor_copy(
+            wsd[:].rearrange("p (t m) -> p m t", t=PACK), ws[:].rearrange("p (m t) -> p m t", t=PACK)
+        )
+        xq = held([P, S], U32, "xq")
+        nc.vector.tensor_copy(xq[:], xw[:].indirect(lists["offs"][:]))
+
+        ybank = []
+        for t in range(PACK):
+            bank = psum.tile([P, 512], F32, name="y%d" % t, tag="bank%d" % (2 * t + 1))
+            nc.tensor.matmul_mx(
+                out=bank[:],
+                lhsT=wd[:, 256 * t : 256 * (t + 1)].bitcast(FP4X4),
+                lhsT_scale=wsd[:, P * t : P * (t + 1)],
+                rhs=xq[:].bitcast(FP8X4),
+                rhs_scale=xqs[:],
+                start=True,
+                stop=True,
+            )
+            ybank.append(bank)
+
+        ypos = [held([P, S], F32, "ypos%d" % t) for t in range(PACK)]
+        yga = [held([P, S], F32, "yga%d" % t) for t in range(PACK)]
+        pair = [held([P, 2 * S], F32, "pair%d" % t) for t in range(PACK)]
+
+        def relu_out(t):
+            nc.scalar.activation(ypos[t][:], ybank[t][:], RELU)
+
+        def neg_out(t):
+            nc.scalar.activation(pair[t][:, :S], ybank[t][:], COPY, scale=-1.0)
+
+        def fetch_n4(t):
+            for h in range(2):
+                nc.vector.tensor_copy(
+                    pair[t][:, S + HALF * h : S + HALF * (h + 1)], ypos[t][:].indirect(entries(lists["n4"], HALF * h, HALF))
+                )
+
+        def put_n3(t):
+            nc.vector.tensor_tensor(pg[t][:].indirect(lists["n3"][:]), pair[t][:, :S], pair[t][:, S:], ADD)
+
+        relu_out(0)
+        fetch_n4(0)
+        for t in range(1, PACK):
+            relu_out(t)
+            neg_out(t - 1)
+            fetch_n4(t)
+            put_n3(t - 1)
+        for t in range(PACK):
+            nc.scalar.activation(yga[t][:], ybank[t][:], COPY, scale=ga_sb[:, t : t + 1])
+        neg_out(PACK - 1)
+        put_n3(PACK - 1)
+
+        z2c = held([P, PACK, U], BF16, "z2c")
+        for t in range(PACK):
+            nc.scalar.activation(z2c[:, t, :], pg[t][:], COPY, scale=gb_sb[:, t : t + 1])
+        z2b = [held([P, 512 * PACK], BF16, "z2b%d" % h) for h in range(2)]
+        for h in range(2):
+            nc.scalar.copy(
+                z2b[h][:].rearrange("p (c i t) -> p c t i", i=4, t=PACK),
+                z2c[:, :, 512 * h : 512 * (h + 1)].rearrange("p t (c i) -> p c t i", i=4),
+            )
+
+        diff = [held([P, PACK, HALF], F32, "diff%d" % h) for h in range(2)]
+        units = [(h, t) for h in range(2) for t in range(PACK)]
+
+        def fetch_n1(h, t):
+            nc.vector.tensor_copy(
+                pair[PACK - 1][:, HALF * t : HALF * (t + 1)], yga[t][:].indirect(entries(lists["n1"], HALF * h, HALF))
+            )
+
+        def fetch_n2(h, t):
+            nc.vector.tensor_tensor(
+                diff[h][:, t, :],
+                yga[t][:].indirect(entries(lists["n2"], HALF * h, HALF)),
+                pair[PACK - 1][:, HALF * t : HALF * (t + 1)],
+                SUB,
+            )
+
+        fetch_n1(*units[0])
+        for u in range(1, len(units)):
+            fetch_n1(*units[u])
+            fetch_n2(*units[u - 1])
+        fetch_n2(*units[-1])
+
+        zb = held([P, PACK, P, PACK], BF16, "zb")
+        for h in range(2):
+            nc.scalar.copy(
+                zb[:, :, 64 * h : 64 * (h + 1), :].rearrange("p r m j -> p m j r"),
+                diff[h][:].rearrange("p j (m r) -> p m j r", r=PACK),
+            )
+
+        z2q = [held([P, 512], U32, "z2q%d" % h) for h in range(2)]
+        z2s = [held([P, 512], U8, "z2s%d" % h) for h in range(2)]
+        for h in range(2):
+            nc.vector.quantize_mx(out=z2q[h][:].bitcast(FP8X4), scales=z2s[h][:], in_=z2b[h][:])
+        zq = [held([P, P], U32, "zq%d" % r) for r in range(PACK)]
+        zs = [held([P, P], U8, "zs%d" % r) for r in range(PACK)]
+        for r in range(PACK):
+            nc.vector.quantize_mx(
+                out=zq[r][:].bitcast(FP8X4), scales=zs[r][:], in_=zb[:, r, :, :].rearrange("p m j -> p (m j)")
+            )
+
+        sbank = {}
+        for r in range(PACK):
+            for h in range(2):
+                bank = psum.tile([P, 512], F32, name="s%d_%d" % (r, h), tag="bank%d" % (2 * r + h))
+                nc.tensor.matmul_mx(
+                    out=bank[:],
+                    lhsT=zq[r][:].bitcast(FP8X4),
+                    lhsT_scale=zs[r][:],
+                    rhs=z2q[h][:].bitcast(FP8X4),
+                    rhs_scale=z2s[h][:],
+                    start=True,
+                    stop=True,
+                )
+                sbank[r, h] = bank
+
+        win = [held([P, U], F32, "win%d" % r) for r in range(PACK)]
+        neg = {(r, h): held([P, 512], F32, "neg%d_%d" % (r, h)) for r in range(PACK) for h in range(2)}
+        for r in range(PACK):
+            nc.scalar.activation(win[r][:, :512], sbank[r, 0][:], COPY, scale=0.75 * 0.0625)
+            if r == 0:
+                nc.vector.tensor_scalar_mul(win[r][:, 512:], sbank[r, 1][:], 0.75 * 0.0625)
+            else:
+                nc.scalar.activation(win[r][:, 512:], sbank[r, 1][:], COPY, scale=0.75 * 0.0625)
+            nc.scalar.activation(neg[r, 0][:], sbank[r, 0][:], COPY, scale=-0.0625)
+        for r in range(PACK):
+            nc.scalar.activation(neg[r, 1][:], sbank[r, 1][:], COPY, scale=-0.0625)
+
+        pieces = [(0, 512), (512, 256), (768, 256)]
+        res = [held([P, PACK, n], F32, "res%d" % c) for c, (w0, n) in enumerate(pieces)]
+        steps = [(c, r, w) for c, (w0, n) in enumerate(pieces) for r in range(PACK) for w in range(w0, w0 + n, HALF)]
+        part = {}
+        rows_out = out_0.rearrange("(p r) w -> p r w", r=PACK)
+        words_out = out_1[0].rearrange("p n t -> p (n t)").bitcast(I32)
+        oscale = held([P, U], U8, "oscale")
+
+        def fetch_n5(c, r, w):
+            part[r, w] = ring.tile([P, HALF], F32, name="part", align_bytes=64)
+            nc.vector.tensor_tensor(
+                part[r, w][:],
+                win[r][:].indirect(entries(lists["n5"], w, HALF)),
+                neg[r, w // 512][:, w % 512 : w % 512 + HALF],
+                ADD,
+            )
+
+        def fetch_n6(c, r, w):
+            w0, n = pieces[c]
+            nc.vector.tensor_tensor(
+                res[c][:, r, w - w0 : w - w0 + HALF], win[r][:].indirect(entries(lists["n6"], w, HALF)), part[r, w][:], ADD
+            )
+            if w + HALF == w0 + n:
+                nc.sync.dma_start(rows_out[:, r, w0 : w0 + n], res[c][:, r, :])
+                if r == PACK - 1:
+                    rounded = held([P, n * PACK], BF16, "rounded%d" % c)
+                    woven = rounded[:].rearrange("p (c i r) -> p c r i", i=4, r=PACK)
+                    planes = res[c][:].rearrange("p r (c i) -> p c r i", i=4)
+                    if c < len(pieces) - 1:
+                        nc.scalar.copy(woven, planes)
+                    else:
+                        nc.scalar.copy(woven[:, :24], planes[:, :24])
+                        nc.vector.tensor_copy(woven[:, 24:], planes[:, 24:])
+                    codes = held([P, n], U32, "codes%d" % c)
+                    nc.vector.quantize_mx(out=codes[:].bitcast(FP8X4), scales=oscale[:, w0 : w0 + n], in_=rounded[:])
+                    nc.sync.dma_start(words_out[:, w0 : w0 + n], codes[:].bitcast(I32))
+
+        fetch_n5(*steps[0])
+        for u in range(1, len(steps)):
+            fetch_n5(*steps[u])
+            fetch_n6(*steps[u - 1])
+        fetch_n6(*steps[-1])
+        for q in range(4):
+            queue = nc.sync if q % 2 == 0 else nc.scalar
+            queue.dma_start(out_2[0][4 * q : 4 * q + 4, :].bitcast(I32), oscale[32 * q : 32 * q + 4, :].bitcast(I32))

@@ -50,7 +50,7 @@ def tile_picked_selfgappagezlap_none_po_kernel(
         gb_sb = held([P, PACK], F32, "gb_sb")
         pg = [held([P, U], F32, "pg%d" % t) for t in range(PACK)]
 
-        nc.gpsimd.memset(xs[:].bitcast(I32), 0)
+        nc.vector.memset(xs[:].bitcast(I32), 0)
         nc.gpsimd.memset(ws[:].bitcast(I32), 0)
         nc.sync.dma_start(lists["offs"][:], offs)
         nc.sync.dma_start(ww[:].bitcast(I32), w1_words[0].bitcast(I32))
@@ -80,51 +80,55 @@ def tile_picked_selfgappagezlap_none_po_kernel(
             wsd[:].rearrange("p (t m) -> p m t", t=PACK), ws[:].rearrange("p (m t) -> p m t", t=PACK)
         )
         xq = held([P, S], U32, "xq")
-        nc.vector.tensor_copy(xq[:], xw[:].indirect(lists["offs"][:]))
-
-        ybank = []
-        for t in range(PACK):
-            bank = psum.tile([P, 512], F32, name="y%d" % t, tag="bank%d" % (2 * t + 1))
-            nc.tensor.matmul_mx(
-                out=bank[:],
-                lhsT=wd[:, 256 * t : 256 * (t + 1)].bitcast(FP4X4),
-                lhsT_scale=wsd[:, P * t : P * (t + 1)],
-                rhs=xq[:].bitcast(FP8X4),
-                rhs_scale=xqs[:],
-                start=True,
-                stop=True,
+        for h in range(2):
+            nc.vector.tensor_copy(
+                xq[:, HALF * h : HALF * (h + 1)], xw[:].indirect(entries(lists["offs"], HALF * h, HALF))
             )
-            ybank.append(bank)
 
-        ypos = [held([P, S], F32, "ypos%d" % t) for t in range(PACK)]
-        yga = [held([P, S], F32, "yga%d" % t) for t in range(PACK)]
-        pair = [held([P, 2 * S], F32, "pair%d" % t) for t in range(PACK)]
+        spans = [[(0, HALF), (HALF, HALF)]] + [[(0, S)]] * (PACK - 1)
+        ybank = {}
+        for t in range(PACK):
+            for j0, n in spans[t]:
+                bank = psum.tile([P, 512], F32, name="y%d_%d" % (t, j0), tag="bank%d" % (2 * t + j0 // HALF))
+                nc.tensor.matmul_mx(
+                    out=bank[:, :n],
+                    lhsT=wd[:, 256 * t : 256 * (t + 1)].bitcast(FP4X4),
+                    lhsT_scale=wsd[:, P * t : P * (t + 1)],
+                    rhs=xq[:, j0 : j0 + n].bitcast(FP8X4),
+                    rhs_scale=xqs[:, j0 : j0 + n],
+                    start=True,
+                    stop=True,
+                )
+                ybank[t, j0] = bank
 
-        def relu_out(t):
-            nc.scalar.activation(ypos[t][:], ybank[t][:], RELU)
+        def empty(t, dst, func, scale):
+            for j0, n in spans[t]:
+                nc.scalar.activation(dst[:, j0 : j0 + n], ybank[t, j0][:, :n], func, scale=scale)
 
-        def neg_out(t):
-            nc.scalar.activation(pair[t][:, :S], ybank[t][:], COPY, scale=-1.0)
+        pos_win = [held([P, S if t == 0 else 2 * S], F32, "pos_win%d" % t) for t in range(PACK)]
+        ga_win = [held([P, S], F32, "ga_win%d" % t) for t in range(PACK)]
+        own = [held([P, S], F32, "fetched%d" % t) for t in range(PACK - 1)]
+        last = held([P, 2 * S], F32, "last")
+        yneg = [pos_win[1][:, S:], pos_win[2][:, S:], pos_win[3][:, S:], last[:, :S]]
+        fetched = [own[0][:], own[1][:], own[2][:], last[:, S:]]
 
         def fetch_n4(t):
-            for h in range(2):
-                nc.vector.tensor_copy(
-                    pair[t][:, S + HALF * h : S + HALF * (h + 1)], ypos[t][:].indirect(entries(lists["n4"], HALF * h, HALF))
-                )
+            for j0, n in spans[t]:
+                nc.vector.tensor_copy(fetched[t][:, j0 : j0 + n], pos_win[t][:].indirect(entries(lists["n4"], j0, n)))
 
         def put_n3(t):
-            nc.vector.tensor_tensor(pg[t][:].indirect(lists["n3"][:]), pair[t][:, :S], pair[t][:, S:], ADD)
+            nc.vector.tensor_tensor(pg[t][:].indirect(lists["n3"][:]), yneg[t], fetched[t], ADD)
 
-        relu_out(0)
+        empty(0, pos_win[0], RELU, 1.0)
         fetch_n4(0)
         for t in range(1, PACK):
-            relu_out(t)
-            neg_out(t - 1)
+            empty(t, pos_win[t], RELU, 1.0)
+            empty(t - 1, yneg[t - 1], COPY, -1.0)
             fetch_n4(t)
             put_n3(t - 1)
         for t in range(PACK):
-            nc.scalar.activation(yga[t][:], ybank[t][:], COPY, scale=ga_sb[:, t : t + 1])
-        neg_out(PACK - 1)
+            empty(t, ga_win[t], COPY, ga_sb[:, t : t + 1])
+        empty(PACK - 1, yneg[PACK - 1], COPY, -1.0)
         put_n3(PACK - 1)
 
         z2c = held([P, PACK, U], BF16, "z2c")
@@ -142,14 +146,14 @@ def tile_picked_selfgappagezlap_none_po_kernel(
 
         def fetch_n1(h, t):
             nc.vector.tensor_copy(
-                pair[PACK - 1][:, HALF * t : HALF * (t + 1)], yga[t][:].indirect(entries(lists["n1"], HALF * h, HALF))
+                last[:, HALF * t : HALF * (t + 1)], ga_win[t][:].indirect(entries(lists["n1"], HALF * h, HALF))
             )
 
         def fetch_n2(h, t):
             nc.vector.tensor_tensor(
                 diff[h][:, t, :],
-                yga[t][:].indirect(entries(lists["n2"], HALF * h, HALF)),
-                pair[PACK - 1][:, HALF * t : HALF * (t + 1)],
+                ga_win[t][:].indirect(entries(lists["n2"], HALF * h, HALF)),
+                last[:, HALF * t : HALF * (t + 1)],
                 SUB,
             )
 
@@ -200,46 +204,40 @@ def tile_picked_selfgappagezlap_none_po_kernel(
                 nc.vector.tensor_scalar_mul(win[r][:, 512:], sbank[r, 1][:], 0.75 * 0.0625)
             else:
                 nc.scalar.activation(win[r][:, 512:], sbank[r, 1][:], COPY, scale=0.75 * 0.0625)
-            nc.scalar.activation(neg[r, 0][:], sbank[r, 0][:], COPY, scale=-0.0625)
-        for r in range(PACK):
-            nc.scalar.activation(neg[r, 1][:], sbank[r, 1][:], COPY, scale=-0.0625)
+            for h in range(2):
+                nc.scalar.activation(neg[r, h][:], sbank[r, h][:], COPY, scale=-0.0625)
 
         pieces = [(0, 512), (512, 256), (768, 256)]
         res = [held([P, PACK, n], F32, "res%d" % c) for c, (w0, n) in enumerate(pieces)]
-        steps = [(c, r, w) for c, (w0, n) in enumerate(pieces) for r in range(PACK) for w in range(w0, w0 + n, HALF)]
+        steps = [(c, r) for r in range(PACK) for c in range(2)] + [(2, r) for r in range(PACK)]
         part = {}
         rows_out = out_0.rearrange("(p r) w -> p r w", r=PACK)
         words_out = out_1[0].rearrange("p n t -> p (n t)").bitcast(I32)
         oscale = held([P, U], U8, "oscale")
 
-        def fetch_n5(c, r, w):
-            part[r, w] = ring.tile([P, HALF], F32, name="part", align_bytes=64)
+        def fetch_n5(c, r):
+            w0, n = pieces[c]
+            part[c, r] = ring.tile([P, n], F32, name="part", align_bytes=64)
             nc.vector.tensor_tensor(
-                part[r, w][:],
-                win[r][:].indirect(entries(lists["n5"], w, HALF)),
-                neg[r, w // 512][:, w % 512 : w % 512 + HALF],
+                part[c, r][:],
+                win[r][:].indirect(entries(lists["n5"], w0, n)),
+                neg[r, w0 // 512][:, w0 % 512 : w0 % 512 + n],
                 ADD,
             )
 
-        def fetch_n6(c, r, w):
+        def fetch_n6(c, r):
             w0, n = pieces[c]
-            nc.vector.tensor_tensor(
-                res[c][:, r, w - w0 : w - w0 + HALF], win[r][:].indirect(entries(lists["n6"], w, HALF)), part[r, w][:], ADD
-            )
-            if w + HALF == w0 + n:
-                nc.sync.dma_start(rows_out[:, r, w0 : w0 + n], res[c][:, r, :])
-                if r == PACK - 1:
-                    rounded = held([P, n * PACK], BF16, "rounded%d" % c)
-                    woven = rounded[:].rearrange("p (c i r) -> p c r i", i=4, r=PACK)
-                    planes = res[c][:].rearrange("p r (c i) -> p c r i", i=4)
-                    if c < len(pieces) - 1:
-                        nc.scalar.copy(woven, planes)
-                    else:
-                        nc.scalar.copy(woven[:, :24], planes[:, :24])
-                        nc.vector.tensor_copy(woven[:, 24:], planes[:, 24:])
-                    codes = held([P, n], U32, "codes%d" % c)
-                    nc.vector.quantize_mx(out=codes[:].bitcast(FP8X4), scales=oscale[:, w0 : w0 + n], in_=rounded[:])
-                    nc.sync.dma_start(words_out[:, w0 : w0 + n], codes[:].bitcast(I32))
+            nc.vector.tensor_tensor(res[c][:, r, :], win[r][:].indirect(entries(lists["n6"], w0, n)), part[c, r][:], ADD)
+            nc.sync.dma_start(rows_out[:, r, w0 : w0 + n], res[c][:, r, :])
+            if r == PACK - 1:
+                rounded = held([P, n * PACK], BF16, "rounded%d" % c)
+                nc.scalar.copy(
+                    rounded[:].rearrange("p (c i r) -> p c r i", i=4, r=PACK),
+                    res[c][:].rearrange("p r (c i) -> p c r i", i=4),
+                )
+                codes = held([P, n], U32, "codes%d" % c)
+                nc.vector.quantize_mx(out=codes[:].bitcast(FP8X4), scales=oscale[:, w0 : w0 + n], in_=rounded[:])
+                nc.sync.dma_start(words_out[:, w0 : w0 + n], codes[:].bitcast(I32))
 
         fetch_n5(*steps[0])
         for u in range(1, len(steps)):

@@ -32,25 +32,25 @@ def tile_picked_selfgappagezlap_none_po_kernel(
     nc = tc.nc
     with ExitStack() as ctx:
         keep = ctx.enter_context(tc.tile_pool(name="keep", bufs=1))
+        reuse = ctx.enter_context(tc.tile_pool(name="reuse", bufs=1))
         ring = ctx.enter_context(tc.tile_pool(name="ring", bufs=3))
         psum = ctx.enter_context(tc.psum_pool(name="psum", bufs=1))
 
-        def held(shape, dtype, name):
-            return keep.tile(shape, dtype, name=name, align_bytes=64)
+        def held(shape, dtype, name, tag=""):
+            return keep.tile(shape, dtype, name=name, tag=tag or name, align_bytes=64)
 
         lists = {}
         for name, src in (("offs", offs), ("n4", n4), ("n3", n3), ("n1", n1), ("n2", n2), ("n5", n5), ("n6", n6)):
             lists[name] = held(list(src.shape), U16, "list_" + name)
 
         xw = held([P, T], U32, "xw")
-        xs = held([P, T], U8, "xs")
+        xs = reuse.tile([P, T], U8, name="xs", align_bytes=64, offset=0)
         ww = held([P, 2 * H], U8, "ww")
-        ws = held([P, H], U8, "ws")
+        ws = reuse.tile([P, H], U8, name="ws", align_bytes=64, offset=T)
         ga_sb = held([P, PACK], F32, "ga_sb")
         gb_sb = held([P, PACK], F32, "gb_sb")
-        pg = [held([P, U], F32, "pg%d" % t) for t in range(PACK)]
 
-        nc.vector.memset(xs[:].bitcast(I32), 0)
+        nc.gpsimd.memset(xs[:].bitcast(I32), 0)
         nc.gpsimd.memset(ws[:].bitcast(I32), 0)
         nc.sync.dma_start(lists["offs"][:], offs)
         nc.sync.dma_start(ww[:].bitcast(I32), w1_words[0].bitcast(I32))
@@ -66,8 +66,6 @@ def tile_picked_selfgappagezlap_none_po_kernel(
         nc.sync.dma_start(gb_sb[:], gb.rearrange("(p t) o -> p (t o)", t=PACK))
         for name, src in (("n1", n1), ("n2", n2), ("n5", n5), ("n6", n6)):
             nc.sync.dma_start(lists[name][:], src)
-        for t in range(PACK):
-            nc.vector.memset(pg[t][:], 0.0)
 
         wd = held([P, 2 * H], U8, "wd")
         nc.vector.tensor_copy(
@@ -79,7 +77,7 @@ def tile_picked_selfgappagezlap_none_po_kernel(
         nc.vector.tensor_copy(
             wsd[:].rearrange("p (t m) -> p m t", t=PACK), ws[:].rearrange("p (m t) -> p m t", t=PACK)
         )
-        xq = held([P, S], U32, "xq")
+        xq = reuse.tile([P, S], U32, name="xq", align_bytes=64, offset=T // 2)
         for h in range(2):
             nc.vector.tensor_copy(
                 xq[:, HALF * h : HALF * (h + 1)], xw[:].indirect(entries(lists["offs"], HALF * h, HALF))
@@ -100,6 +98,10 @@ def tile_picked_selfgappagezlap_none_po_kernel(
                     stop=True,
                 )
                 ybank[t, j0] = bank
+
+        pg = [held([P, U], F32, "pg%d" % t, tag) for t, tag in enumerate(("xw", "wd", "wsd", "xqs"))]
+        for t in range(PACK):
+            nc.gpsimd.memset(pg[t][:], 0.0)
 
         def empty(t, dst, func, scale):
             for j0, n in spans[t]:
@@ -198,46 +200,54 @@ def tile_picked_selfgappagezlap_none_po_kernel(
 
         win = [held([P, U], F32, "win%d" % r) for r in range(PACK)]
         neg = {(r, h): held([P, 512], F32, "neg%d_%d" % (r, h)) for r in range(PACK) for h in range(2)}
+        nc.scalar.activation(win[0][:, :512], sbank[0, 0][:], COPY, scale=0.75 * 0.0625)
+        nc.vector.tensor_scalar_mul(win[0][:, 512:], sbank[0, 1][:], 0.75 * 0.0625)
         for r in range(PACK):
-            nc.scalar.activation(win[r][:, :512], sbank[r, 0][:], COPY, scale=0.75 * 0.0625)
-            if r == 0:
-                nc.vector.tensor_scalar_mul(win[r][:, 512:], sbank[r, 1][:], 0.75 * 0.0625)
-            else:
-                nc.scalar.activation(win[r][:, 512:], sbank[r, 1][:], COPY, scale=0.75 * 0.0625)
             for h in range(2):
                 nc.scalar.activation(neg[r, h][:], sbank[r, h][:], COPY, scale=-0.0625)
+            if r > 0:
+                for h in range(2):
+                    nc.scalar.activation(win[r][:, 512 * h : 512 * (h + 1)], sbank[r, h][:], COPY, scale=0.75 * 0.0625)
 
         pieces = [(0, 512), (512, 256), (768, 256)]
         res = [held([P, PACK, n], F32, "res%d" % c) for c, (w0, n) in enumerate(pieces)]
-        steps = [(c, r) for r in range(PACK) for c in range(2)] + [(2, r) for r in range(PACK)]
+        steps = [(0, 0, 0, HALF), (0, 0, HALF, HALF), (1, 0, 512, HALF)]
+        steps = steps + [(c, r) + pieces[c] for r in range(1, PACK) for c in range(2)]
+        steps = steps + [(2, r) + pieces[2] for r in range(PACK)]
         part = {}
         rows_out = out_0.rearrange("(p r) w -> p r w", r=PACK)
         words_out = out_1[0].rearrange("p n t -> p (n t)").bitcast(I32)
         oscale = held([P, U], U8, "oscale")
 
-        def fetch_n5(c, r):
-            w0, n = pieces[c]
-            part[c, r] = ring.tile([P, n], F32, name="part", align_bytes=64)
+        def fetch_n5(c, r, w, n):
+            part[r, w] = ring.tile([P, n], F32, name="part", align_bytes=64)
             nc.vector.tensor_tensor(
-                part[c, r][:],
-                win[r][:].indirect(entries(lists["n5"], w0, n)),
-                neg[r, w0 // 512][:, w0 % 512 : w0 % 512 + n],
+                part[r, w][:],
+                win[r][:].indirect(entries(lists["n5"], w, n)),
+                neg[r, w // 512][:, w % 512 : w % 512 + n],
                 ADD,
             )
 
-        def fetch_n6(c, r):
-            w0, n = pieces[c]
-            nc.vector.tensor_tensor(res[c][:, r, :], win[r][:].indirect(entries(lists["n6"], w0, n)), part[c, r][:], ADD)
-            nc.sync.dma_start(rows_out[:, r, w0 : w0 + n], res[c][:, r, :])
+        def fetch_n6(c, r, w, n):
+            w0, width = pieces[c]
+            nc.vector.tensor_tensor(
+                res[c][:, r, w - w0 : w - w0 + n], win[r][:].indirect(entries(lists["n6"], w, n)), part[r, w][:], ADD
+            )
+            if w + n < w0 + width:
+                return
+            nc.sync.dma_start(rows_out[:, r, w0 : w0 + width], res[c][:, r, :])
             if r == PACK - 1:
-                rounded = held([P, n * PACK], BF16, "rounded%d" % c)
-                nc.scalar.copy(
-                    rounded[:].rearrange("p (c i r) -> p c r i", i=4, r=PACK),
-                    res[c][:].rearrange("p r (c i) -> p c r i", i=4),
-                )
-                codes = held([P, n], U32, "codes%d" % c)
-                nc.vector.quantize_mx(out=codes[:].bitcast(FP8X4), scales=oscale[:, w0 : w0 + n], in_=rounded[:])
-                nc.sync.dma_start(words_out[:, w0 : w0 + n], codes[:].bitcast(I32))
+                rounded = held([P, width * PACK], BF16, "rounded%d" % c)
+                woven = rounded[:].rearrange("p (c i r) -> p c r i", i=4, r=PACK)
+                planes = res[c][:].rearrange("p r (c i) -> p c r i", i=4)
+                if c < len(pieces) - 1:
+                    nc.scalar.copy(woven, planes)
+                else:
+                    nc.scalar.copy(woven[:, :40], planes[:, :40])
+                    nc.vector.tensor_copy(woven[:, 40:], planes[:, 40:])
+                codes = held([P, width], U32, "codes%d" % c)
+                nc.vector.quantize_mx(out=codes[:].bitcast(FP8X4), scales=oscale[:, w0 : w0 + width], in_=rounded[:])
+                nc.sync.dma_start(words_out[:, w0 : w0 + width], codes[:].bitcast(I32))
 
         fetch_n5(*steps[0])
         for u in range(1, len(steps)):

from contextlib import ExitStack

import concourse.mybir as mybir

F32 = mybir.dt.float32
BF16 = mybir.dt.bfloat16
I32 = mybir.dt.int32
U32 = mybir.dt.uint32
U16 = mybir.dt.uint16
U8 = mybir.dt.uint8
FP8X4 = mybir.dt.float8_e4m3fn_x4
FP4X4 = mybir.dt.float4_e2m1fn_x4
ADD = mybir.AluOpType.add
SUB = mybir.AluOpType.subtract
COPY = mybir.ActivationFunctionType.Copy
RELU = mybir.ActivationFunctionType.Relu

P = 128
K, T, S, H, U = 512, 2048, 512, 512, 1024
PACK = 4
HALF = 256
FLOPS = 2 * K * H * S + 2 * H * S * U


def entries(tile, first, count):
    return tile[:, first // 16 : (first + count) // 16]


def tile_picked_selfgappagezlap_none_po_kernel(
    tc, x_words, x_scales, w1_words, w1_scales, ga, gb, offs, n1, n2, n3, n4, n5, n6, out_0, out_1, out_2
):
    nc = tc.nc
    with ExitStack() as ctx:
        keep = ctx.enter_context(tc.tile_pool(name="keep", bufs=1))
        reuse = ctx.enter_context(tc.tile_pool(name="reuse", bufs=1))
        ring = ctx.enter_context(tc.tile_pool(name="ring", bufs=3))
        psum = ctx.enter_context(tc.psum_pool(name="psum", bufs=1))

        def held(shape, dtype, name, tag=""):
            return keep.tile(shape, dtype, name=name, tag=tag or name, align_bytes=64)

        lists = {}
        for name, src in (("offs", offs), ("n4", n4), ("n3", n3), ("n1", n1), ("n2", n2), ("n5", n5), ("n6", n6)):
            lists[name] = held(list(src.shape), U16, "list_" + name)

        xw = held([P, T], U32, "xw")
        xs = reuse.tile([P, T], U8, name="xs", align_bytes=64, offset=0)
        ww = held([P, 2 * H], U8, "ww")
        ws = reuse.tile([P, H], U8, name="ws", align_bytes=64, offset=T)
        ga_sb = held([P, PACK], F32, "ga_sb")
        gb_sb = held([P, PACK], F32, "gb_sb")

        nc.gpsimd.memset(xs[:].bitcast(I32), 0)
        nc.gpsimd.memset(ws[:].bitcast(I32), 0)
        nc.sync.dma_start(lists["offs"][:], offs)
        nc.sync.dma_start(ww[:].bitcast(I32), w1_words[0].bitcast(I32))
        nc.sync.dma_start(xw[:].bitcast(I32), x_words[0].rearrange("p n t -> p (n t)").bitcast(I32))
        for q in range(4):
            nc.scalar.dma_start(xs[32 * q : 32 * q + 4, :].bitcast(I32), x_scales[0][4 * q : 4 * q + 4, :].bitcast(I32))
        for q in range(4):
            queue = nc.scalar if q < 2 else nc.gpsimd
            queue.dma_start(ws[32 * q : 32 * q + 4, :].bitcast(I32), w1_scales[0][4 * q : 4 * q + 4, :].bitcast(I32))
        nc.sync.dma_start(lists["n4"][:], n4)
        nc.sync.dma_start(lists["n3"][:], n3)
        nc.sync.dma_start(ga_sb[:], ga.rearrange("(p t) o -> p (t o)", t=PACK))
        nc.sync.dma_start(gb_sb[:], gb.rearrange("(p t) o -> p (t o)", t=PACK))
        for name, src in (("n1", n1), ("n2", n2), ("n5", n5), ("n6", n6)):
            nc.sync.dma_start(lists[name][:], src)

        wd = held([P, 2 * H], U8, "wd")
        nc.vector.tensor_copy(
            wd[:].rearrange("p (t m b) -> p m t b", t=PACK, b=2), ww[:].rearrange("p (m t b) -> p m t b", t=PACK, b=2)
        )
        xqs = held([P, S], U8, "xqs")
        nc.vector.tensor_copy(xqs[:], xs[:].indirect(lists["offs"][:]))
        wsd = held([P, H], U8, "wsd")
        nc.vector.tensor_copy(
            wsd[:].rearrange("p (t m) -> p m t", t=PACK), ws[:].rearrange("p (m t) -> p m t", t=PACK)
        )
        xq = reuse.tile([P, S], U32, name="xq", align_bytes=64, offset=T // 2)
        for h in range(2):
            nc.vector.tensor_copy(
                xq[:, HALF * h : HALF * (h + 1)], xw[:].indirect(entries(lists["offs"], HALF * h, HALF))
            )

        spans = [[(0, HALF), (HALF, HALF)]] + [[(0, S)]] * (PACK - 1)
        ybank = {}
        for t in range(PACK):
            for j0, n in spans[t]:
                bank = psum.tile([P, 512], F32, name="y%d_%d" % (t, j0), tag="bank%d" % (2 * t + j0 // HALF))
                nc.tensor.matmul_mx(
                    out=bank[:, :n],
                    lhsT=wd[:, 256 * t : 256 * (t + 1)].bitcast(FP4X4),
                    lhsT_scale=wsd[:, P * t : P * (t + 1)],
                    rhs=xq[:, j0 : j0 + n].bitcast(FP8X4),
                    rhs_scale=xqs[:, j0 : j0 + n],
                    start=True,
                    stop=True,
                )
                ybank[t, j0] = bank

        pg = [held([P, U], F32, "pg%d" % t, tag) for t, tag in enumerate(("xw", "wd", "wsd", "xqs"))]
        for t in range(PACK):
            nc.gpsimd.memset(pg[t][:], 0.0)

        def empty(t, dst, func, scale):
            for j0, n in spans[t]:
                nc.scalar.activation(dst[:, j0 : j0 + n], ybank[t, j0][:, :n], func, scale=scale)

        pos_win = [held([P, S if t == 0 else 2 * S], F32, "pos_win%d" % t) for t in range(PACK)]
        ga_win = [held([P, S], F32, "ga_win%d" % t) for t in range(PACK)]
        own = [held([P, S], F32, "fetched%d" % t) for t in range(PACK - 1)]
        last = held([P, 2 * S], F32, "last")
        yneg = [pos_win[1][:, S:], pos_win[2][:, S:], pos_win[3][:, S:], last[:, :S]]
        fetched = [own[0][:], own[1][:], own[2][:], last[:, S:]]

        def fetch_n4(t):
            for j0, n in spans[t]:
                nc.vector.tensor_copy(fetched[t][:, j0 : j0 + n], pos_win[t][:].indirect(entries(lists["n4"], j0, n)))

        def put_n3(t):
            nc.vector.tensor_tensor(pg[t][:].indirect(lists["n3"][:]), yneg[t], fetched[t], ADD)

        empty(0, pos_win[0], RELU, 1.0)
        fetch_n4(0)
        for t in range(1, PACK):
            empty(t, pos_win[t], RELU, 1.0)
            empty(t - 1, yneg[t - 1], COPY, -1.0)
            fetch_n4(t)
            put_n3(t - 1)
        for t in range(PACK):
            empty(t, ga_win[t], COPY, ga_sb[:, t : t + 1])
        empty(PACK - 1, yneg[PACK - 1], COPY, -1.0)
        put_n3(PACK - 1)

        z2c = held([P, PACK, U], BF16, "z2c")
        for t in range(PACK):
            nc.scalar.activation(z2c[:, t, :], pg[t][:], COPY, scale=gb_sb[:, t : t + 1])
        z2b = [held([P, 512 * PACK], BF16, "z2b%d" % h) for h in range(2)]
        for h in range(2):
            nc.scalar.copy(
                z2b[h][:].rearrange("p (c i t) -> p c t i", i=4, t=PACK),
                z2c[:, :, 512 * h : 512 * (h + 1)].rearrange("p t (c i) -> p c t i", i=4),
            )

        diff = [held([P, PACK, HALF], F32, "diff%d" % h) for h in range(2)]
        units = [(h, t) for h in range(2) for t in range(PACK)]

        def fetch_n1(h, t):
            nc.vector.tensor_copy(
                last[:, HALF * t : HALF * (t + 1)], ga_win[t][:].indirect(entries(lists["n1"], HALF * h, HALF))
            )

        def fetch_n2(h, t):
            nc.vector.tensor_tensor(
                diff[h][:, t, :],
                ga_win[t][:].indirect(entries(lists["n2"], HALF * h, HALF)),
                last[:, HALF * t : HALF * (t + 1)],
                SUB,
            )

        fetch_n1(*units[0])
        for u in range(1, len(units)):
            fetch_n1(*units[u])
            fetch_n2(*units[u - 1])
        fetch_n2(*units[-1])

        zb = held([P, PACK, P, PACK], BF16, "zb")
        for h in range(2):
            nc.scalar.copy(
                zb[:, :, 64 * h : 64 * (h + 1), :].rearrange("p r m j -> p m j r"),
                diff[h][:].rearrange("p j (m r) -> p m j r", r=PACK),
            )

        z2q = [held([P, 512], U32, "z2q%d" % h) for h in range(2)]
        z2s = [held([P, 512], U8, "z2s%d" % h) for h in range(2)]
        for h in range(2):
            nc.vector.quantize_mx(out=z2q[h][:].bitcast(FP8X4), scales=z2s[h][:], in_=z2b[h][:])
        zq = [held([P, P], U32, "zq%d" % r) for r in range(PACK)]
        zs = [held([P, P], U8, "zs%d" % r) for r in range(PACK)]
        for r in range(PACK):
            nc.vector.quantize_mx(
                out=zq[r][:].bitcast(FP8X4), scales=zs[r][:], in_=zb[:, r, :, :].rearrange("p m j -> p (m j)")
            )

        sbank = {}
        for r in range(PACK):
            for h in range(2):
                bank = psum.tile([P, 512], F32, name="s%d_%d" % (r, h), tag="bank%d" % (2 * r + h))
                nc.tensor.matmul_mx(
                    out=bank[:],
                    lhsT=zq[r][:].bitcast(FP8X4),
                    lhsT_scale=zs[r][:],
                    rhs=z2q[h][:].bitcast(FP8X4),
                    rhs_scale=z2s[h][:],
                    start=True,
                    stop=True,
                )
                sbank[r, h] = bank

        win = [held([P, U], F32, "win%d" % r) for r in range(PACK)]
        neg = {(r, h): held([P, 512], F32, "neg%d_%d" % (r, h)) for r in range(PACK) for h in range(2)}
        nc.scalar.activation(win[0][:, :512], sbank[0, 0][:], COPY, scale=0.75 * 0.0625)
        nc.vector.tensor_scalar_mul(win[0][:, 512:], sbank[0, 1][:], 0.75 * 0.0625)
        for r in range(PACK):
            for h in range(2):
                nc.scalar.activation(neg[r, h][:], sbank[r, h][:], COPY, scale=-0.0625)
            if r > 0:
                for h in range(2):
                    nc.scalar.activation(win[r][:, 512 * h : 512 * (h + 1)], sbank[r, h][:], COPY, scale=0.75 * 0.0625)

        pieces = [(0, 512), (512, 256), (768, 256)]
        res = [held([P, PACK, n], F32, "res%d" % c) for c, (w0, n) in enumerate(pieces)]
        steps = [(0, 0, 0, HALF), (0, 0, HALF, HALF), (1, 0, 512, HALF)]
        steps = steps + [(c, r) + pieces[c] for r in range(1, PACK) for c in range(2)]
        steps = steps + [(2, r) + pieces[2] for r in range(PACK)]
        part = {}
        rows_out = out_0.rearrange("(p r) w -> p r w", r=PACK)
        words_out = out_1[0].rearrange("p n t -> p (n t)").bitcast(I32)
        oscale = held([P, U], U8, "oscale")

        def fetch_n5(c, r, w, n):
            part[r, w] = ring.tile([P, n], F32, name="part", align_bytes=64)
            nc.vector.tensor_tensor(
                part[r, w][:],
                win[r][:].indirect(entries(lists["n5"], w, n)),
                neg[r, w // 512][:, w % 512 : w % 512 + n],
                ADD,
            )

        def fetch_n6(c, r, w, n):
            w0, width = pieces[c]
            nc.vector.tensor_tensor(
                res[c][:, r, w - w0 : w - w0 + n], win[r][:].indirect(entries(lists["n6"], w, n)), part[r, w][:], ADD
            )
            if w + n < w0 + width:
                return
            nc.sync.dma_start(rows_out[:, r, w0 : w0 + width], res[c][:, r, :])
            if r == PACK - 1:
                rounded = held([P, width * PACK], BF16, "rounded%d" % c)
                woven = rounded[:].rearrange("p (c i r) -> p c r i", i=4, r=PACK)
                planes = res[c][:].rearrange("p r (c i) -> p c r i", i=4)
                if c < len(pieces) - 1:
                    nc.scalar.copy(woven, planes)
                else:
                    nc.scalar.copy(woven[:, :40], planes[:, :40])
                    nc.vector.tensor_copy(woven[:, 40:], planes[:, 40:])
                codes = held([P, width], U32, "codes%d" % c)
                nc.vector.quantize_mx(out=codes[:].bitcast(FP8X4), scales=oscale[:, w0 : w0 + width], in_=rounded[:])
                nc.sync.dma_start(words_out[:, w0 : w0 + width], codes[:].bitcast(I32))

        fetch_n5(*steps[0])
        for u in range(1, len(steps)):
            fetch_n5(*steps[u])
            fetch_n6(*steps[u - 1])
        fetch_n6(*steps[-1])
        for q in range(4):
            queue = nc.sync if q % 2 == 0 else nc.scalar
            queue.dma_start(out_2[0][4 * q : 4 * q + 4, :].bitcast(I32), oscale[32 * q : 32 * q + 4, :].bitcast(I32))
